import numpy as np
import ml_dtypes


def mxq(x, axis, fmt="e4m3"):
    dtype, down = {"e4m3": (ml_dtypes.float8_e4m3fn, 7), "e5m2": (ml_dtypes.float8_e5m2, 14)}[fmt]
    v = np.moveaxis(np.asarray(x, np.float32).astype(ml_dtypes.bfloat16).astype(np.float64), axis, -1)
    blocks = v.reshape(v.shape[:-1] + (-1, 32))
    amax = np.abs(blocks).max(-1, keepdims=True)
    byte = np.maximum(np.where(amax > 0, np.frexp(amax)[1] - 1 + 127, 0) - down, 1)
    scale = np.exp2(byte - 127.0)
    codes = (blocks / scale).astype(np.float32).astype(dtype).astype(np.float64)
    return np.moveaxis((codes * scale).reshape(v.shape), -1, axis)


WIDE = False


def mx_kscale(k):
    if not WIDE:
        return np.ones(k)
    levels = np.array([10, -10, 5, -5, 0])
    if k % 512:
        return np.exp2(np.random.permutation(np.resize(levels, k // 32))).repeat(32)
    a = np.empty((k // 512, 16))
    for p in range(k // 512):
        a[p, :8] = np.random.permutation(np.resize(levels, 8))
        for g in range(8):
            far = levels[np.abs(levels - a[p, g]) >= 10]
            a[p, g + 8] = far[np.random.randint(len(far))]
    return np.exp2(a.ravel()).repeat(32)


BF16 = ml_dtypes.bfloat16


def bf(x):
    return np.asarray(x, np.float32).astype(BF16)


def f64(x):
    return np.asarray(x).astype(np.float64)


E2M1 = np.array([0.0, 0.5, 1.0, 1.5, 2.0, 3.0, 4.0, 6.0, -0.0, -0.5, -1.0, -1.5, -2.0, -3.0, -4.0, -6.0])


def pack_weight(w, fmt):
    k, n = w.shape
    w = f64(bf(w)).reshape(k // 32, 32, n)
    amax = np.abs(w).max(1)
    if fmt == "e4m3":
        byte = np.frexp(amax)[1] - 1 + 127 - 7
    else:
        mant, ex = np.frexp(amax / 6.0)
        byte = np.where(mant > 0.5, ex, ex - 1) + 127
    byte = np.clip(np.where(amax > 0, byte, 1), 1, 254)
    scaled = (w * np.exp2(127.0 - byte)[:, None, :]).reshape(k, n).astype(np.float32)
    by_word = np.ascontiguousarray(scaled.reshape(k // 512, 128, 4, n).transpose(0, 1, 3, 2))
    if fmt == "e4m3":
        words = by_word.astype(ml_dtypes.float8_e4m3fn).view(np.uint8)
    else:
        c = by_word.astype(ml_dtypes.float4_e2m1fn).view(np.uint8) & 0xF
        words = c[..., 0::2] | (c[..., 1::2] << 4)
    return np.ascontiguousarray(words), np.ascontiguousarray(byte.astype(np.uint8).reshape(k // 512, 16, n))


def unpack_weight(words, scales, fmt):
    g, p, n, _ = words.shape
    if fmt == "e4m3":
        vals = np.ascontiguousarray(words).view(ml_dtypes.float8_e4m3fn).astype(np.float64)
    else:
        nib = np.empty((g, p, n, 4), np.uint8)
        nib[..., 0::2] = words & 0xF
        nib[..., 1::2] = words >> 4
        vals = E2M1[nib]
    vals = vals * np.repeat(np.exp2(scales.astype(np.float64) - 127.0), 8, axis=1)[..., None]
    return vals.transpose(0, 1, 3, 2).reshape(g * 512, n)

def planes(Y):
    n, m = Y.shape
    b = f64(bf(Y)).reshape(n // 32, 32, m)
    amax = np.abs(b).max(1)
    byte = np.clip(np.where(amax > 0, np.frexp(amax)[1] - 1 + 127 - 7, 1), 1, 254)
    codes = (b * np.exp2(127.0 - byte)[:, None, :]).reshape(n, m).astype(np.float32).astype(ml_dtypes.float8_e4m3fn).view(np.uint8)
    words = codes.reshape(n // 512, 128, 4, m).transpose(0, 1, 3, 2)
    return np.ascontiguousarray(words), np.ascontiguousarray(byte.astype(np.uint8).reshape(n // 512, 16, m))


B, R, S, C = 2, 1024, 1024, 512


def setup_inputs():
    s = mx_kscale(C)
    t = mx_kscale(S)
    q = bf(np.random.standard_normal((B, R, C)) * s)
    kc = bf(np.random.standard_normal((B, S, C)) / s)
    n_words, n_scales = pack_weight(np.random.standard_normal((C, C)) / np.sqrt(C) * s[:, None], "e4m3")
    return {"q": q,
            "kc": kc,
            "n_words": n_words,
            "n_scales": n_scales,
            "beta": bf((1.0 + 0.1 * np.random.standard_normal(C)) * s),
            "sv": bf(np.random.uniform(0.5, 1.5, (B, S)) / t),
            "g": bf(np.random.standard_normal(S) * 0.375 * np.sqrt(S) * t)}


def attention_weights(qq, kq):
    s = (qq @ kq.transpose(0, 2, 1)) / np.sqrt(C)
    e = np.exp(s - s.max(-1, keepdims=True))
    return e / e.sum(-1, keepdims=True)


def values_from_keys(kc, kq, nq, beta, sv):
    u = kq @ nq
    return sv[:, :, None] * (beta[None, None, :] * kc + u)


def core(q, kc, n_words, n_scales, beta, sv, g):
    k = f64(kc)
    kq = mxq(k, 2, "e4m3")
    p = attention_weights(mxq(f64(q), 2, "e4m3"), kq)
    a = p * f64(g)[None, None, :]
    v = values_from_keys(k, kq, unpack_weight(n_words, n_scales, "e4m3"), f64(beta), f64(sv))
    return mxq(a, 2, "e4m3") @ mxq(v, 1, "e4m3")


def reference(q, kc, n_words, n_scales, beta, sv, g):
    R_out = core(q, kc, n_words, n_scales, beta, sv, g)
    words, scales = planes(np.moveaxis(R_out, 2, 0).reshape(512, -1))
    return R_out, words, scales

@@ -1,0 +1,446 @@
+from contextlib import ExitStack
+import math
+
+import concourse.mybir as mybir
+from concourse.masks import make_identity
+
+F32 = mybir.dt.float32
+BF16 = mybir.dt.bfloat16
+I32 = mybir.dt.int32
+U32 = mybir.dt.uint32
+U8 = mybir.dt.uint8
+FP8X4 = mybir.dt.float8_e4m3fn_x4
+ALU = mybir.AluOpType
+ACT = mybir.ActivationFunctionType
+AX = mybir.AxisListType
+
+B, R, S, C = 2, 1024, 1024, 512
+P = 128
+NT = B * R // P
+SCALE = 1.0 / math.sqrt(C)
+FLOPS = 2 * B * R * S * C * 2 + 2 * B * S * C * C
+
+
+def tile_mfakeyreusevaluedecode_x2_kernel(tc, q, kc, n_words, n_scales, beta, sv, g, out_0, out_1, out_2):
+    nc = tc.nc
+    with ExitStack() as ctx:
+        keep = ctx.enter_context(tc.tile_pool(name="keep", bufs=1))
+        work = ctx.enter_context(tc.tile_pool(name="work", bufs=2))
+        ps = ctx.enter_context(tc.psum_pool(name="ps", bufs=1))
+        banks = {"s": 3, "m": 2, "a": 1, "o": 1, "t": 1}
+
+        def kt(shape, dt, name):
+            return keep.tile(shape, dt, name=name, tag=name, align_bytes=64)
+
+        def wt(shape, dt, name, bufs):
+            return work.tile(shape, dt, name=name, tag=name, bufs=bufs, align_bytes=64)
+
+        kc_sb = {}
+        q_sb = {}
+
+        def load_kc(b, gg, pieces):
+            rows = kc[b, 512 * gg : 512 * (gg + 1), :].rearrange("(p j) c -> p j c", j=4)
+            n = 4 // pieces
+            for i in range(pieces):
+                t = kt([P, n, C], BF16, "kc_%d%d%d" % (b, gg, i))
+                nc.sync.dma_start(out=t[:], in_=rows[:, n * i : n * (i + 1), :])
+                for h in range(2):
+                    if pieces == 1 or h == i:
+                        kc_sb[b, gg, h] = t[:, 2 * h : 2 * h + 2, :] if pieces == 1 else t[:]
+
+        def load_q(pair):
+            t = kt([P, 2, C], BF16, "q_%d" % pair)
+            b, r0 = divmod(256 * pair, R)
+            nc.sync.dma_start(out=t[:], in_=q[b, r0 : r0 + 256, :].rearrange("(i p) c -> p i c", p=P))
+            q_sb[pair] = t[:]
+
+        rows_z = kt([P, 3 * S], BF16, "rows_z")
+        ones = kt([P, P], BF16, "ones")
+        n_raw = kt([P, C], U32, "n_raw")
+        n_sraw = kt([P, C], U8, "n_sraw")
+        n_codes = kt([P, C], U32, "n_codes")
+        n_sc = kt([P, C], U8, "n_sc")
+        beta_sb = kt([P, 4], BF16, "beta_sb")
+        ident = kt([P, P], F32, "ident")
+        scr = kt([P, 1], F32, "scr")
+
+        nc.gpsimd.memset(n_sraw[:].bitcast(I32), 0)
+        make_identity(nc, ident[:])
+        nc.vector.memset(scr[:], 0.0)
+        nc.vector.memset(rows_z[:].bitcast(I32), 0)
+        nc.vector.memset(ones[:], 1.0)
+        dummy = kt([P, 1], F32, "dummy")
+        nc.scalar.activation(out=dummy[:], in_=scr[:], func=ACT.Exp)
+
+        load_kc(0, 0, 2)
+        for qd in range(4):
+            nc.sync.dma_start(out=n_sraw[32 * qd : 32 * qd + 4, :].bitcast(I32), in_=n_scales[0, 4 * qd : 4 * qd + 4, :].bitcast(I32))
+        load_kc(0, 1, 1)
+        load_q(0)
+        nc.sync.dma_start(out=n_raw[:].bitcast(I32), in_=n_words[0].rearrange("p n t -> p (n t)").bitcast(I32))
+        nc.sync.dma_start(out=rows_z[0:1, 0:S], in_=g.rearrange("(o t) -> o t", o=1))
+        nc.sync.dma_start(out=rows_z[0:1, S : 3 * S], in_=sv.rearrange("b t -> (b t)").rearrange("(o t) -> o t", o=1))
+        nc.sync.dma_start(out=beta_sb[:], in_=beta.rearrange("(p j) -> p j", j=4))
+        load_q(1)
+        load_q(2)
+        load_q(3)
+        load_kc(1, 0, 1)
+        load_kc(1, 1, 1)
+        for pair in range(4, 8):
+            load_q(pair)
+
+        def n_perm():
+            nc.vector.tensor_copy(out=n_codes[:].bitcast(I32).rearrange("p (j m) -> p j m", j=4), in_=n_raw[:].bitcast(I32).rearrange("p (m j) -> p j m", j=4))
+
+        nc.gpsimd.tensor_copy(out=n_sc[:].rearrange("p (j m) -> p m j", j=4), in_=n_sraw[:].rearrange("p (m j) -> p m j", j=4))
+
+        def bank(name):
+            return ps.tile([P, 512], F32, name=name, tag=name, bufs=banks[name])
+
+        def copy_on(eng):
+            return nc.scalar.copy if eng == "s" else nc.vector.tensor_copy
+
+        kcT = {}
+        kq = {}
+        qT = {}
+        qq = {}
+        for b in range(B):
+            for gg in range(2):
+                kcT[b, gg] = kt([P, 2048], BF16, "kcT_%d%d" % (b, gg))
+                kq[b, gg] = (kt([P, 512], U32, "kq_%d%d" % (b, gg)), kt([P, 512], U8, "kqs_%d%d" % (b, gg)))
+
+        def turn(src):
+            t = bank("m")
+            words = src.bitcast(F32)
+            for i in range(2):
+                for u in range(2):
+                    nc.tensor.transpose(t[:, 256 * i + 128 * u : 256 * i + 128 * (u + 1)], words[:, i, u:256:2], ident[:])
+            return t
+
+        def unturn(t, dst_words, eng):
+            copy_on(eng)(out=dst_words.rearrange("p (i r u) -> p i r u", i=2, u=2), in_=t[:].rearrange("p (i u r) -> p i r u", i=2, u=2))
+
+        def kc_turn(b, gg, h):
+            return turn(kc_sb[b, gg, h])
+
+        def kc_copy(b, gg, h, t, eng):
+            unturn(t, kcT[b, gg][:].bitcast(F32)[:, 512 * h : 512 * (h + 1)], eng)
+
+        def kc_quant(b, gg):
+            c, s = kq[b, gg]
+            nc.vector.quantize_mx(out=c[:].bitcast(FP8X4), scales=s[:], in_=kcT[b, gg][:])
+
+        def q_turn(pair):
+            return turn(q_sb[pair])
+
+        def q_copy(pair, t, eng):
+            qT[pair] = wt([P, 1024], BF16, "qT", 3)
+            unturn(t, qT[pair][:].bitcast(F32), eng)
+
+        def q_quant(pair):
+            qq[pair] = (kt([P, 256], U32, "qq_%d" % pair), kt([P, 256], U8, "qqs_%d" % pair))
+            nc.vector.quantize_mx(out=qq[pair][0][:].bitcast(FP8X4), scales=qq[pair][1][:], in_=qT[pair][:])
+
+        bc = {}
+
+        def spread(i):
+            t = bank("m")
+            nc.tensor.matmul(t[:], lhsT=ones[:], rhs=rows_z[:, 512 * i : 512 * (i + 1)], start=True, stop=True)
+            return t
+
+        bct = kt([P, 3 * S], BF16, "bct")
+
+        def spread_copy(i, t, eng):
+            copy_on(eng)(
+                out=bct[:, 512 * i : 512 * (i + 1)].rearrange("p (u m e) -> p u m e", u=2, e=2),
+                in_=t[:].rearrange("p (m u e) -> p u m e", u=2, e=2),
+            )
+
+        vT = {}
+        vg = {}
+        vq = {}
+        xt = {}
+        ub = {}
+        for b in range(B):
+            vT[b] = kt([P, 4, S], BF16, "vT_%d" % b)
+            for gg in range(2):
+                vq[b, gg] = (kt([P, 512], U32, "vq_%d%d" % (b, gg)), kt([P, 512], U8, "vqs_%d%d" % (b, gg)))
+
+        def u_mm(b, gg, j):
+            t = bank("m")
+            c, s = kq[b, gg]
+            nc.tensor.matmul_mx(
+                out=t[:],
+                lhsT=n_codes[:, 128 * j : 128 * (j + 1)].bitcast(FP8X4),
+                lhsT_scale=n_sc[:, 128 * j : 128 * (j + 1)],
+                rhs=c[:].bitcast(FP8X4),
+                rhs_scale=s[:],
+                start=True,
+                stop=True,
+            )
+            ub[b, gg, j] = t
+
+        def x_stt(b, gg, j):
+            x = wt([P, 512], F32, "x", 4)
+            nc.vector.scalar_tensor_tensor(
+                out=x[:], in0=kcT[b, gg][:, j:2048:4], scalar=beta_sb[:, j : j + 1], in1=ub[b, gg, j][:], op0=ALU.mult, op1=ALU.add
+            )
+            xt[b, gg, j] = x
+
+        def x_sv(b, gg, j):
+            nc.vector.tensor_tensor(
+                out=vT[b][:, j, 512 * gg : 512 * (gg + 1)].rearrange("p (u m e) -> p u m e", u=2, e=2),
+                in0=xt[b, gg, j][:].rearrange("p (u e m) -> p u m e", u=2, e=2),
+                in1=bct[:, S * (1 + b) + 512 * gg : S * (1 + b) + 512 * (gg + 1)].rearrange("p (u m e) -> p u m e", u=2, e=2),
+                op=ALU.mult,
+            )
+
+        def v_turn(b, gg, jp):
+            t = bank("m")
+            words = vT[b][:].bitcast(F32)
+            for jj in range(2):
+                for u in range(2):
+                    w0 = 256 * gg + 128 * u
+                    nc.tensor.transpose(t[:, 256 * jj + 128 * u : 256 * jj + 128 * (u + 1)], words[:, 2 * jp + jj, w0 : w0 + 128], ident[:])
+            return t
+
+        def v_copy(b, gg, jp, t, eng):
+            if jp == 0:
+                vg[b, gg] = wt([P, 2048], BF16, "vg", 2)
+            unturn(t, vg[b, gg][:].bitcast(F32)[:, 512 * jp : 512 * (jp + 1)], eng)
+
+        def v_quant(b, gg):
+            c, s = vq[b, gg]
+            nc.vector.quantize_mx(out=c[:].bitcast(FP8X4), scales=s[:], in_=vg[b, gg][:])
+
+        sb = {}
+        et = {}
+        at = {}
+        aT = {}
+        aq = {}
+        bias = {}
+        tot = {}
+        ob = {}
+
+        def scores(k):
+            b = k // 8
+            qc, qs = qq[k // 2]
+            cols = slice(128 * (k % 2), 128 * (k % 2) + 128)
+            sb[k] = []
+            for gg in range(2):
+                t = bank("s")
+                c, s = kq[b, gg]
+                nc.tensor.matmul_mx(
+                    out=t[:], lhsT=qc[:, cols].bitcast(FP8X4), lhsT_scale=qs[:, cols], rhs=c[:].bitcast(FP8X4), rhs_scale=s[:], start=True, stop=True
+                )
+                sb[k].append(t)
+
+        mxt = {}
+
+        def rowmax(k):
+            mx = wt([P, 2], F32, "mx", 3)
+            mxt[k] = mx
+            for gg in range(2):
+                nc.vector.tensor_reduce(out=mx[:, gg : gg + 1], in_=sb[k][gg][:], axis=AX.X, op=ALU.max)
+
+        def shift(k):
+            mx = mxt[k]
+            bias[k] = wt([P, 1], F32, "bias", 3)
+            nc.vector.tensor_scalar(out=bias[k][:], in0=mx[:, 0:1], scalar1=mx[:, 1:2], scalar2=-SCALE, op0=ALU.max, op1=ALU.mult)
+
+        def expo(k):
+            et[k] = wt([P, S], F32, "e", 3)
+            sm = wt([P, 2], F32, "sm", 3)
+            for gg in range(2):
+                nc.scalar.activation(
+                    out=et[k][:, 512 * gg : 512 * (gg + 1)].rearrange("p (u m e) -> p u m e", u=2, e=2),
+                    in_=sb[k][gg][:].rearrange("p (u e m) -> p u m e", u=2, e=2),
+                    func=ACT.Exp,
+                    bias=bias[k][:],
+                    scale=SCALE,
+                    accum_out=sm[:, gg : gg + 1],
+                )
+            tot[k] = wt([P, 1], F32, "tot", 3)
+            nc.scalar.activation(out=tot[k][:], in_=sm[:, 0:1], func=ACT.Identity, bias=sm[:, 1:2])
+
+        rit = {}
+
+        def rec(k):
+            rit[k] = wt([P, 1], F32, "ri", 3)
+            nc.vector.reciprocal(out=rit[k][:], in_=tot[k][:])
+
+        def weights(k):
+            ri = rit[k]
+            at[k] = wt([P, S], BF16, "a", 3)
+            nc.vector.scalar_tensor_tensor(out=at[k][:], in0=et[k][:], scalar=ri[:], in1=bct[:, 0:S], op0=ALU.mult, op1=ALU.mult)
+
+        def a_turn(k):
+            t = bank("a")
+            words = at[k][:].bitcast(F32)
+            for i in range(4):
+                nc.tensor.transpose(t[:, 128 * i : 128 * (i + 1)], words[:, 128 * i : 128 * (i + 1)], ident[:])
+            aT[k] = t
+
+        ag = {}
+
+        def a_copy(k, eng):
+            ag[k] = wt([P, 1024], BF16, "ag", 3)
+            unturn(aT[k], ag[k][:].bitcast(F32), eng)
+
+        def a_quant(k):
+            aq[k] = (wt([P, 256], U32, "aq", 4), wt([P, 256], U8, "aqs", 4))
+            nc.vector.quantize_mx(out=aq[k][0][:].bitcast(FP8X4), scales=aq[k][1][:], in_=ag[k][:])
+
+        def outs_mm(k):
+            b = k // 8
+            ac, as_ = aq[k]
+            o = bank("o")
+            for gg in range(2):
+                c, s = vq[b, gg]
+                cols = slice(128 * gg, 128 * gg + 128)
+                nc.tensor.matmul_mx(
+                    out=o[:], lhsT=ac[:, cols].bitcast(FP8X4), lhsT_scale=as_[:, cols], rhs=c[:].bitcast(FP8X4), rhs_scale=s[:], start=(gg == 0), stop=(gg == 1)
+                )
+            oT = bank("t")
+            for j in range(4):
+                jc = slice(128 * j, 128 * j + 128)
+                for gg in range(2):
+                    c, s = vq[b, gg]
+                    cols = slice(128 * gg, 128 * gg + 128)
+                    nc.tensor.matmul_mx(
+                        out=oT[:, jc], lhsT=c[:, jc].bitcast(FP8X4), lhsT_scale=s[:, jc], rhs=ac[:, cols].bitcast(FP8X4), rhs_scale=as_[:, cols], start=(gg == 0), stop=(gg == 1)
+                    )
+            ob[k] = (o, oT)
+
+        groups = [(0, 4), (4, 4), (8, 4), (12, 2), (14, 1), (15, 1)]
+        group_of = {}
+        for k0, n in groups:
+            for k in range(k0, k0 + n):
+                group_of[k] = (k0, n)
+        pg = {}
+
+        def outs_copy0(k, eng0):
+            o = ob[k][0]
+            b, i = divmod(k, 8)
+            os_ = wt([P, C], F32, "os", 4)
+            copy_on(eng0)(out=os_[:].rearrange("p (m j) -> p m j", j=4), in_=o[:].rearrange("p (j m) -> p m j", j=4))
+            nc.sync.dma_start(out=out_0[b, 128 * i : 128 * (i + 1), :], in_=os_[:])
+
+        def outs_copy1(k, eng1):
+            oT = ob[k][1]
+            k0, n = group_of[k]
+            if k == k0:
+                pg[k0] = wt([P, 512 * n], BF16, "pg%d" % n, 2)
+            copy_on(eng1)(
+                out=pg[k0][:, 512 * (k - k0) : 512 * (k - k0 + 1)].rearrange("p (r j) -> p r j", j=4), in_=oT[:].rearrange("p (j r) -> p r j", j=4)
+            )
+
+        def planes(k):
+            k0, n = group_of[k]
+            if k != k0 + n - 1:
+                return
+            w = 128 * n
+            pc = wt([P, w], U32, "pc%d" % n, 2)
+            psc = wt([P, w], U8, "psc%d" % n, 2)
+            nc.vector.quantize_mx(out=pc[:].bitcast(FP8X4), scales=psc[:], in_=pg[k0][:])
+            m0 = 128 * k0
+            nc.sync.dma_start(out=out_1[0, :, m0 : m0 + w, :].rearrange("p m t -> p (m t)").bitcast(I32), in_=pc[:].bitcast(I32))
+            for qd in range(4):
+                nc.sync.dma_start(out=out_2[0, 4 * qd : 4 * qd + 4, m0 : m0 + w].bitcast(I32), in_=psc[32 * qd : 32 * qd + 4, :].bitcast(I32))
+
+        units = [(b, gg, j) for b in range(B) for gg in range(2) for j in range(4)]
+        unit_at = {-1: [0, 1, 2], 0: [3, 4, 5], 1: [6, 7], 3: [8], 4: [9, 10], 5: [11, 12], 6: [13], 7: [14, 15]}
+        vturn_at = {0: [0], 1: [1, 2], 2: [3], 5: [4], 6: [5], 7: [6], 8: [7]}
+        kc_at = {0: [0, 1], 2: [2, 3]}
+        q_at = {0: 2, 2: 3, 4: 4, 6: 5, 8: 6, 10: 7}
+        outs_at = {k: [k - 1] for k in range(1, NT + 1)}
+        outs_at[1] = []
+        outs_at[2] = []
+        outs_at[3] = [0, 1, 2]
+        spread_at = {1: [4], 3: [5]}
+        kc_parts = [(1, 0, 0), (1, 0, 1), (1, 1, 0), (1, 1, 1)]
+        v_parts = [(b, gg, jp) for b in range(B) for gg in range(2) for jp in range(2)]
+
+        ta = kc_turn(0, 0, 0)
+        tb = kc_turn(0, 0, 1)
+        kc_copy(0, 0, 0, ta, "s")
+        kc_copy(0, 0, 1, tb, "v")
+        ta = kc_turn(0, 1, 0)
+        tb = kc_turn(0, 1, 1)
+        kc_copy(0, 1, 0, ta, "s")
+        kc_copy(0, 1, 1, tb, "v")
+        ta = q_turn(0)
+        q_copy(0, ta, "s")
+        kc_quant(0, 0)
+        kc_quant(0, 1)
+        q_quant(0)
+        n_perm()
+        scores(0)
+        for i in range(4):
+            ta = spread(i)
+            spread_copy(i, ta, "s")
+        for u in unit_at[-1]:
+            u_mm(*units[u])
+
+        ta = q_turn(1)
+        q_copy(1, ta, "s")
+        pend = [(q_quant, (1,))]
+        for k in range(-1, NT + 3):
+            late = k >= NT - 1
+            if 0 <= k + 2 < NT:
+                scores(k + 2)
+            todo = []
+            for i in kc_at.get(k, []):
+                todo.append((kc_copy, kc_parts[i], kc_turn(*kc_parts[i])))
+            if k in q_at:
+                todo.append((q_copy, (q_at[k],), q_turn(q_at[k])))
+            for i in vturn_at.get(k, []):
+                todo.append((v_copy, v_parts[i], v_turn(*v_parts[i])))
+            for i in spread_at.get(k, []):
+                todo.append((spread_copy, (i,), spread(i)))
+            if k + 1 < NT:
+                rowmax(k + 1)
+            if 0 <= k < NT:
+                rec(k)
+            if 0 <= k - 1 < NT:
+                a_copy(k - 1, "s")
+            for u in unit_at.get(k, [])[:1]:
+                x_stt(*units[u])
+            if k + 1 < NT:
+                shift(k + 1)
+            for u in unit_at.get(k, [])[1:]:
+                x_stt(*units[u])
+            for i in outs_at.get(k - 1, []):
+                outs_copy0(i, "s")
+            for fn, a, t in todo[:1]:
+                fn(*a, t, "s")
+            if k + 1 < NT:
+                expo(k + 1)
+            for i in outs_at.get(k - 1, []):
+                outs_copy1(i, "v" if late else "s")
+            for fn, a, t in todo[1:]:
+                fn(*a, t, "s")
+            if 0 <= k < NT:
+                weights(k)
+            for fn, a in pend:
+                fn(*a)
+            pend = []
+            for u in unit_at.get(k, []):
+                x_sv(*units[u])
+            if 0 <= k - 1 < NT:
+                a_quant(k - 1)
+            for i in outs_at.get(k - 1, []):
+                planes(i)
+            for i in kc_at.get(k, [])[1::2]:
+                pend.append((kc_quant, kc_parts[i][:2]))
+            if k in q_at:
+                pend.append((q_quant, (q_at[k],)))
+            for i in vturn_at.get(k, []):
+                if i % 2 == 1:
+                    pend.append((v_quant, v_parts[i][:2]))
+            for i in outs_at.get(k, []):
+                outs_mm(i)
+            for u in unit_at.get(k + 1, []):
+                u_mm(*units[u])
+            if 0 <= k < NT:
+                a_turn(k)

@@ -1,5 +1,5 @@
-from contextlib import ExitStack
 import math
+from contextlib import ExitStack
 
 import concourse.mybir as mybir
 from concourse.masks import make_identity
@@ -16,9 +16,32 @@ AX = mybir.AxisListType
 
 B, R, S, C = 2, 1024, 1024, 512
 P = 128
-NT = B * R // P
+HALF = 512
+HALVES = S // HALF
+TILES = B * R // P
+TILES_PER_BATCH = R // P
 SCALE = 1.0 / math.sqrt(C)
 FLOPS = 2 * B * R * S * C * 2 + 2 * B * S * C * C
+
+QUERY_STEP = [None, 0, 2, 4, 5, 5, 7, 11]
+KEY_STEP = [2, 3, 5, 6]
+VALUE_STEP = [-2, -2, 0, 0, 1, 1, 2, 3, 3, 4, 4, 5, 6, 7, 9, 10]
+VALUE_GROUP_STEP = [1, 4, 8, 11]
+GAIN_STEP = 0
+OUT_STEP = [7, 8, 9, 9, 10, 11, 12, 12, 13, 14, 15, 15, 16, 17, 18, 19]
+FIRST_STEP, LAST_STEP = min(VALUE_STEP), max(OUT_STEP)
+VECTOR_COPY_TILES = (11, 12, 14, 15)
+PLANE_GROUPS = [(0, 4), (4, 4), (8, 4), (12, 2), (14, 1), (15, 1)]
+
+BANKS = {"score": 4, "even": 2, "odd": 2}
+
+
+def due(table, step):
+    return [n for n, s in enumerate(table) if s == step]
+
+
+def query_tile(i):
+    return [i] if 0 <= i < TILES else []
 
 
 def tile_mfakeyreusevaluedecode_x2_kernel(tc, q, kc, n_words, n_scales, beta, sv, g, out_0, out_1, out_2):
@@ -26,421 +49,415 @@ def tile_mfakeyreusevaluedecode_x2_kernel(tc, q, kc, n_words, n_scales, beta, sv
     with ExitStack() as ctx:
         keep = ctx.enter_context(tc.tile_pool(name="keep", bufs=1))
         work = ctx.enter_context(tc.tile_pool(name="work", bufs=2))
-        ps = ctx.enter_context(tc.psum_pool(name="ps", bufs=1))
-        banks = {"s": 3, "m": 2, "a": 1, "o": 1, "t": 1}
+        psum = ctx.enter_context(tc.psum_pool(name="psum", bufs=1))
+        ctx.enter_context(tc.manual_schedule())
 
-        def kt(shape, dt, name):
-            return keep.tile(shape, dt, name=name, tag=name, align_bytes=64)
+        def kept(shape, dtype, name):
+            return keep.tile(shape, dtype, name=name, tag=name, align_bytes=64)
 
-        def wt(shape, dt, name, bufs):
-            return work.tile(shape, dt, name=name, tag=name, bufs=bufs, align_bytes=64)
+        def rotating(shape, dtype, name, bufs):
+            return work.tile(shape, dtype, name=name, tag=name, bufs=bufs, align_bytes=64)
 
-        kc_sb = {}
-        q_sb = {}
+        def bank(purpose):
+            return psum.tile([P, 512], F32, name=purpose, tag=purpose, bufs=BANKS[purpose])
 
-        def load_kc(b, gg, pieces):
-            rows = kc[b, 512 * gg : 512 * (gg + 1), :].rearrange("(p j) c -> p j c", j=4)
-            n = 4 // pieces
-            for i in range(pieces):
-                t = kt([P, n, C], BF16, "kc_%d%d%d" % (b, gg, i))
-                nc.sync.dma_start(out=t[:], in_=rows[:, n * i : n * (i + 1), :])
-                for h in range(2):
-                    if pieces == 1 or h == i:
-                        kc_sb[b, gg, h] = t[:, 2 * h : 2 * h + 2, :] if pieces == 1 else t[:]
+        def copy_with(engine):
+            return nc.scalar.copy if engine == "scalar" else nc.vector.tensor_copy
 
-        def load_q(pair):
-            t = kt([P, 2, C], BF16, "q_%d" % pair)
-            b, r0 = divmod(256 * pair, R)
-            nc.sync.dma_start(out=t[:], in_=q[b, r0 : r0 + 256, :].rearrange("(i p) c -> p i c", p=P))
-            q_sb[pair] = t[:]
+        gain_row = kept([P, S], BF16, "gain_row")
+        ident_bf16 = kept([P, P], BF16, "ident_bf16")
+        token_scale_bf16 = kept([P, B * HALVES * 4], BF16, "token_scale_bf16")
+        token_scale = kept([P, B * HALVES * 4], F32, "token_scale")
+        diag = [kept([P, P], BF16, "diag_%d" % j) for j in range(4)]
+        ones = kept([P, P], BF16, "ones")
+        n_codes = kept([P, C], U32, "n_codes")
+        n_scale = kept([P, C], U8, "n_scale")
+        beta_cols = kept([P, 4], BF16, "beta_cols")
+        ident = kept([P, P], F32, "ident")
+        zeros = kept([P, P], BF16, "zeros")
 
-        rows_z = kt([P, 3 * S], BF16, "rows_z")
-        ones = kt([P, P], BF16, "ones")
-        n_raw = kt([P, C], U32, "n_raw")
-        n_sraw = kt([P, C], U8, "n_sraw")
-        n_codes = kt([P, C], U32, "n_codes")
-        n_sc = kt([P, C], U8, "n_sc")
-        beta_sb = kt([P, 4], BF16, "beta_sb")
-        ident = kt([P, P], F32, "ident")
-        scr = kt([P, 1], F32, "scr")
-
-        nc.gpsimd.memset(n_sraw[:].bitcast(I32), 0)
+        nc.gpsimd.memset(n_scale[:].bitcast(I32), 0)
         make_identity(nc, ident[:])
-        nc.vector.memset(scr[:], 0.0)
-        nc.vector.memset(rows_z[:].bitcast(I32), 0)
-        nc.vector.memset(ones[:], 1.0)
-        dummy = kt([P, 1], F32, "dummy")
-        nc.scalar.activation(out=dummy[:], in_=scr[:], func=ACT.Exp)
+        make_identity(nc, ident_bf16[:])
+        nc.vector.memset(zeros[:], 0.0)
+        nc.gpsimd.memset(gain_row[:].bitcast(I32), 0)
+        nc.scalar.activation(out=ones[:], in_=zeros[:], func=ACT.Exp)
 
-        load_kc(0, 0, 2)
-        for qd in range(4):
-            nc.sync.dma_start(out=n_sraw[32 * qd : 32 * qd + 4, :].bitcast(I32), in_=n_scales[0, 4 * qd : 4 * qd + 4, :].bitcast(I32))
-        load_kc(0, 1, 1)
-        load_q(0)
-        nc.sync.dma_start(out=n_raw[:].bitcast(I32), in_=n_words[0].rearrange("p n t -> p (n t)").bitcast(I32))
-        nc.sync.dma_start(out=rows_z[0:1, 0:S], in_=g.rearrange("(o t) -> o t", o=1))
-        nc.sync.dma_start(out=rows_z[0:1, S : 3 * S], in_=sv.rearrange("b t -> (b t)").rearrange("(o t) -> o t", o=1))
-        nc.sync.dma_start(out=beta_sb[:], in_=beta.rearrange("(p j) -> p j", j=4))
-        load_q(1)
-        load_q(2)
-        load_q(3)
-        load_kc(1, 0, 1)
-        load_kc(1, 1, 1)
+        keys = {}
+        queries = {}
+
+        def load_keys(b, h, pieces):
+            rows = kc[b, HALF * h : HALF * (h + 1), :].rearrange("(p j) c -> p j c", j=4)
+            slots = 4 // pieces
+            for piece in range(pieces):
+                t = kept([P, slots, C], BF16, "keys_%d%d%d" % (b, h, piece))
+                nc.sync.dma_start(out=t[:], in_=rows[:, slots * piece : slots * (piece + 1), :])
+                for n in range(slots // 2):
+                    keys[b, h, piece * slots // 2 + n] = t[:, 2 * n : 2 * n + 2, :]
+
+        def load_queries(pair):
+            t = kept([P, 2, C], BF16, "queries_%d" % pair)
+            b, row = divmod(2 * P * pair, R)
+            nc.sync.dma_start(out=t[:], in_=q[b, row : row + 2 * P, :].rearrange("(i p) c -> p i c", p=P))
+            queries[pair] = t[:]
+
+        load_keys(0, 0, 2)
+        load_keys(0, 1, 1)
+        load_queries(0)
+        nc.sync.dma_start(
+            out=token_scale_bf16[:].rearrange("p (a j) -> p a j", j=4),
+            in_=sv.rearrange("b t -> (b t)").rearrange("(a p j) -> p a j", p=P, j=4),
+        )
+        nc.sync.dma_start(out=beta_cols[:], in_=beta.rearrange("(p j) -> p j", j=4))
+        nc.sync.dma_start(out=n_codes[:].bitcast(I32), in_=n_words[0].rearrange("p n t -> p (n t)").bitcast(I32))
+        for quadrant in range(4):
+            nc.sync.dma_start(
+                out=n_scale[32 * quadrant : 32 * quadrant + 4, :].bitcast(I32),
+                in_=n_scales[0, 4 * quadrant : 4 * quadrant + 4, :].bitcast(I32),
+            )
+        nc.sync.dma_start(out=gain_row[0:1, :], in_=g.rearrange("(o t) -> o t", o=1))
+        for pair in range(1, 4):
+            load_queries(pair)
+        load_keys(1, 0, 1)
+        load_keys(1, 1, 1)
         for pair in range(4, 8):
-            load_q(pair)
+            load_queries(pair)
 
-        def n_perm():
-            nc.vector.tensor_copy(out=n_codes[:].bitcast(I32).rearrange("p (j m) -> p j m", j=4), in_=n_raw[:].bitcast(I32).rearrange("p (m j) -> p j m", j=4))
+        def column_constants():
+            nc.vector.tensor_copy(out=token_scale[:], in_=token_scale_bf16[:])
+            for j in range(4):
+                nc.vector.tensor_scalar(out=diag[j][:], in0=ident_bf16[:], scalar1=beta_cols[:, j : j + 1], scalar2=None, op0=ALU.mult)
 
-        nc.gpsimd.tensor_copy(out=n_sc[:].rearrange("p (j m) -> p m j", j=4), in_=n_sraw[:].rearrange("p (m j) -> p m j", j=4))
-
-        def bank(name):
-            return ps.tile([P, 512], F32, name=name, tag=name, bufs=banks[name])
-
-        def copy_on(eng):
-            return nc.scalar.copy if eng == "s" else nc.vector.tensor_copy
-
-        kcT = {}
-        kq = {}
-        qT = {}
-        qq = {}
-        for b in range(B):
-            for gg in range(2):
-                kcT[b, gg] = kt([P, 2048], BF16, "kcT_%d%d" % (b, gg))
-                kq[b, gg] = (kt([P, 512], U32, "kq_%d%d" % (b, gg)), kt([P, 512], U8, "kqs_%d%d" % (b, gg)))
-
-        def turn(src):
-            t = bank("m")
-            words = src.bitcast(F32)
-            for i in range(2):
+        def turn(rows):
+            t = bank("odd")
+            words = rows.bitcast(F32)
+            for n in range(2):
                 for u in range(2):
-                    nc.tensor.transpose(t[:, 256 * i + 128 * u : 256 * i + 128 * (u + 1)], words[:, i, u:256:2], ident[:])
+                    nc.tensor.transpose(t[:, 256 * n + 128 * u : 256 * n + 128 * (u + 1)], words[:, n, u:256:2], ident[:])
             return t
 
-        def unturn(t, dst_words, eng):
-            copy_on(eng)(out=dst_words.rearrange("p (i r u) -> p i r u", i=2, u=2), in_=t[:].rearrange("p (i u r) -> p i r u", i=2, u=2))
-
-        def kc_turn(b, gg, h):
-            return turn(kc_sb[b, gg, h])
-
-        def kc_copy(b, gg, h, t, eng):
-            unturn(t, kcT[b, gg][:].bitcast(F32)[:, 512 * h : 512 * (h + 1)], eng)
-
-        def kc_quant(b, gg):
-            c, s = kq[b, gg]
-            nc.vector.quantize_mx(out=c[:].bitcast(FP8X4), scales=s[:], in_=kcT[b, gg][:])
-
-        def q_turn(pair):
-            return turn(q_sb[pair])
-
-        def q_copy(pair, t, eng):
-            qT[pair] = wt([P, 1024], BF16, "qT", 3)
-            unturn(t, qT[pair][:].bitcast(F32), eng)
-
-        def q_quant(pair):
-            qq[pair] = (kt([P, 256], U32, "qq_%d" % pair), kt([P, 256], U8, "qqs_%d" % pair))
-            nc.vector.quantize_mx(out=qq[pair][0][:].bitcast(FP8X4), scales=qq[pair][1][:], in_=qT[pair][:])
-
-        bc = {}
-
-        def spread(i):
-            t = bank("m")
-            nc.tensor.matmul(t[:], lhsT=ones[:], rhs=rows_z[:, 512 * i : 512 * (i + 1)], start=True, stop=True)
-            return t
-
-        bct = kt([P, 3 * S], BF16, "bct")
-
-        def spread_copy(i, t, eng):
-            copy_on(eng)(
-                out=bct[:, 512 * i : 512 * (i + 1)].rearrange("p (u m e) -> p u m e", u=2, e=2),
-                in_=t[:].rearrange("p (m u e) -> p u m e", u=2, e=2),
+        def join_words(t, out_words, engine):
+            copy_with(engine)(
+                out=out_words.rearrange("p (n r u) -> p n r u", n=2, u=2), in_=t[:].rearrange("p (n u r) -> p n r u", n=2, u=2)
             )
 
-        vT = {}
-        vg = {}
-        vq = {}
-        xt = {}
-        ub = {}
+        key_cols = {}
+        key_mx = {}
+        query_cols = {}
+        query_mx = {}
         for b in range(B):
-            vT[b] = kt([P, 4, S], BF16, "vT_%d" % b)
-            for gg in range(2):
-                vq[b, gg] = (kt([P, 512], U32, "vq_%d%d" % (b, gg)), kt([P, 512], U8, "vqs_%d%d" % (b, gg)))
+            for h in range(HALVES):
+                key_cols[b, h] = kept([P, 4 * HALF], BF16, "key_cols_%d%d" % (b, h))
+                key_mx[b, h] = (kept([P, HALF], U32, "key_codes_%d%d" % (b, h)), kept([P, HALF], U8, "key_scale_%d%d" % (b, h)))
 
-        def u_mm(b, gg, j):
-            t = bank("m")
-            c, s = kq[b, gg]
+        def key_copy(b, h, quarter, t, engine):
+            join_words(t, key_cols[b, h][:].bitcast(F32)[:, 512 * quarter : 512 * (quarter + 1)], engine)
+
+        def key_quantise(b, h):
+            codes, scale = key_mx[b, h]
+            nc.vector.quantize_mx(out=codes[:].bitcast(FP8X4), scales=scale[:], in_=key_cols[b, h][:])
+
+        def query_copy(pair, t):
+            query_cols[pair] = rotating([P, 1024], BF16, "query_cols", 3)
+            join_words(t, query_cols[pair][:].bitcast(F32), "scalar")
+
+        def query_quantise(pair):
+            query_mx[pair] = (kept([P, 256], U32, "query_codes_%d" % pair), kept([P, 256], U8, "query_scale_%d" % pair))
+            codes, scale = query_mx[pair]
+            nc.vector.quantize_mx(out=codes[:].bitcast(FP8X4), scales=scale[:], in_=query_cols[pair][:])
+
+        gain = kept([P, S], BF16, "gain")
+
+        def gain_product(h):
+            t = bank("odd")
+            nc.tensor.matmul(t[:], lhsT=ones[:], rhs=gain_row[:, HALF * h : HALF * (h + 1)], start=True, stop=True)
+            return t
+
+        def gain_copy(h, t):
+            nc.scalar.copy(
+                out=gain[:, HALF * h : HALF * (h + 1)].rearrange("p (u k e) -> p u k e", u=2, e=2),
+                in_=t[:].rearrange("p (k u e) -> p u k e", u=2, e=2),
+            )
+
+        value_slots = [(b, h, j) for b in range(B) for h in range(HALVES) for j in range(4)]
+        value_groups = [(b, h) for b in range(B) for h in range(HALVES)]
+        beta_key = {}
+        scaled_beta_key = {}
+        projection = {}
+        values = {}
+        value_cols = {}
+        value_mx = {}
+        for b, h in value_groups:
+            value_mx[b, h] = (kept([P, C], U32, "value_codes_%d%d" % (b, h)), kept([P, C], U8, "value_scale_%d%d" % (b, h)))
+
+        def beta_key_product(n):
+            b, h, slot = value_slots[n]
+            beta_key[n] = bank("odd")
+            for j in range(4):
+                nc.tensor.matmul(
+                    beta_key[n][:, 128 * j : 128 * (j + 1)],
+                    lhsT=key_cols[b, h][:, 512 * slot + j : 512 * (slot + 1) : 4],
+                    rhs=diag[j][:],
+                    start=True,
+                    stop=True,
+                )
+
+        def beta_key_copy(n):
+            scaled_beta_key[n] = rotating([P, C], F32, "scaled_beta_key", 3)
+            nc.scalar.activation(
+                out=scaled_beta_key[n][:].rearrange("p (m j) -> p m j", j=4),
+                in_=beta_key[n][:].rearrange("p (j m) -> p m j", j=4),
+                func=ACT.Copy,
+                scale=token_scale[:, n : n + 1],
+            )
+
+        def projection_product(n):
+            b, h, slot = value_slots[n]
+            projection[n] = bank("even")
+            codes, scale = key_mx[b, h]
+            cols = slice(128 * slot, 128 * (slot + 1))
             nc.tensor.matmul_mx(
-                out=t[:],
-                lhsT=n_codes[:, 128 * j : 128 * (j + 1)].bitcast(FP8X4),
-                lhsT_scale=n_sc[:, 128 * j : 128 * (j + 1)],
-                rhs=c[:].bitcast(FP8X4),
-                rhs_scale=s[:],
+                out=projection[n][:],
+                lhsT=codes[:, cols].bitcast(FP8X4),
+                lhsT_scale=scale[:, cols],
+                rhs=n_codes[:].bitcast(FP8X4),
+                rhs_scale=n_scale[:],
                 start=True,
                 stop=True,
             )
-            ub[b, gg, j] = t
 
-        def x_stt(b, gg, j):
-            x = wt([P, 512], F32, "x", 4)
+        def value_sum(n):
+            b, h, slot = value_slots[n]
+            if slot == 0:
+                values[b, h] = rotating([P, 4, C], BF16, "values", 2)
             nc.vector.scalar_tensor_tensor(
-                out=x[:], in0=kcT[b, gg][:, j:2048:4], scalar=beta_sb[:, j : j + 1], in1=ub[b, gg, j][:], op0=ALU.mult, op1=ALU.add
-            )
-            xt[b, gg, j] = x
-
-        def x_sv(b, gg, j):
-            nc.vector.tensor_tensor(
-                out=vT[b][:, j, 512 * gg : 512 * (gg + 1)].rearrange("p (u m e) -> p u m e", u=2, e=2),
-                in0=xt[b, gg, j][:].rearrange("p (u e m) -> p u m e", u=2, e=2),
-                in1=bct[:, S * (1 + b) + 512 * gg : S * (1 + b) + 512 * (gg + 1)].rearrange("p (u m e) -> p u m e", u=2, e=2),
-                op=ALU.mult,
+                out=values[b, h][:, slot, :],
+                in0=projection[n][:],
+                scalar=token_scale[:, n : n + 1],
+                in1=scaled_beta_key[n][:],
+                op0=ALU.mult,
+                op1=ALU.add,
             )
 
-        def v_turn(b, gg, jp):
-            t = bank("m")
-            words = vT[b][:].bitcast(F32)
-            for jj in range(2):
-                for u in range(2):
-                    w0 = 256 * gg + 128 * u
-                    nc.tensor.transpose(t[:, 256 * jj + 128 * u : 256 * jj + 128 * (u + 1)], words[:, 2 * jp + jj, w0 : w0 + 128], ident[:])
-            return t
+        def value_interleave(b, h):
+            value_cols[b, h] = rotating([P, 4 * C], BF16, "value_cols", 2)
+            nc.vector.tensor_copy(
+                out=value_cols[b, h][:].rearrange("p (j m t) -> p j m t", j=4, t=4),
+                in_=values[b, h][:].rearrange("p t (m j) -> p j m t", j=4),
+            )
 
-        def v_copy(b, gg, jp, t, eng):
-            if jp == 0:
-                vg[b, gg] = wt([P, 2048], BF16, "vg", 2)
-            unturn(t, vg[b, gg][:].bitcast(F32)[:, 512 * jp : 512 * (jp + 1)], eng)
+        def value_quantise(b, h):
+            codes, scale = value_mx[b, h]
+            nc.vector.quantize_mx(out=codes[:].bitcast(FP8X4), scales=scale[:], in_=value_cols[b, h][:])
 
-        def v_quant(b, gg):
-            c, s = vq[b, gg]
-            nc.vector.quantize_mx(out=c[:].bitcast(FP8X4), scales=s[:], in_=vg[b, gg][:])
+        score = {}
+        half_max = {}
+        shift = {}
+        exps = {}
+        half_sum = {}
+        row_sum = {}
+        inverse = {}
+        weights = {}
+        turned = {}
+        weight_cols = {}
+        weight_mx = {}
 
-        sb = {}
-        et = {}
-        at = {}
-        aT = {}
-        aq = {}
-        bias = {}
-        tot = {}
-        ob = {}
+        def score_product(i, h):
+            codes, scale = query_mx[i // 2]
+            cols = slice(128 * (i % 2), 128 * (i % 2) + 128)
+            key_codes, key_scale = key_mx[i // TILES_PER_BATCH, h]
+            score[i, h] = bank("score")
+            nc.tensor.matmul_mx(
+                out=score[i, h][:],
+                lhsT=codes[:, cols].bitcast(FP8X4),
+                lhsT_scale=scale[:, cols],
+                rhs=key_codes[:].bitcast(FP8X4),
+                rhs_scale=key_scale[:],
+                start=True,
+                stop=True,
+            )
 
-        def scores(k):
-            b = k // 8
-            qc, qs = qq[k // 2]
-            cols = slice(128 * (k % 2), 128 * (k % 2) + 128)
-            sb[k] = []
-            for gg in range(2):
-                t = bank("s")
-                c, s = kq[b, gg]
+        def score_max(i, h):
+            if h == 0:
+                half_max[i] = rotating([P, HALVES], F32, "half_max", 3)
+            nc.vector.tensor_reduce(out=half_max[i][:, h : h + 1], in_=score[i, h][:], axis=AX.X, op=ALU.max)
+
+        def score_shift(i):
+            shift[i] = rotating([P, 1], F32, "shift", 3)
+            nc.vector.tensor_scalar(
+                out=shift[i][:], in0=half_max[i][:, 0:1], scalar1=half_max[i][:, 1:2], scalar2=-SCALE, op0=ALU.max, op1=ALU.mult
+            )
+
+        def exponential(i, h):
+            if h == 0:
+                exps[i] = rotating([P, S], F32, "exps", 3)
+                half_sum[i] = rotating([P, HALVES], F32, "half_sum", 3)
+            nc.scalar.activation(
+                out=exps[i][:, HALF * h : HALF * (h + 1)].rearrange("p (u k e) -> p u k e", u=2, e=2),
+                in_=score[i, h][:].rearrange("p (u e k) -> p u k e", u=2, e=2),
+                func=ACT.Exp,
+                bias=shift[i][:],
+                scale=SCALE,
+                accum_out=half_sum[i][:, h : h + 1],
+            )
+            if h == HALVES - 1:
+                row_sum[i] = rotating([P, 1], F32, "row_sum", 3)
+                nc.gpsimd.tensor_tensor(out=row_sum[i][:], in0=half_sum[i][:, 0:1], in1=half_sum[i][:, 1:2], op=ALU.add)
+
+        def sum_inverse(i):
+            inverse[i] = rotating([P, 1], F32, "inverse", 3)
+            nc.vector.reciprocal(out=inverse[i][:], in_=row_sum[i][:])
+
+        def weight_product(i):
+            weights[i] = rotating([P, S], BF16, "weights", 3)
+            nc.vector.scalar_tensor_tensor(out=weights[i][:], in0=exps[i][:], scalar=inverse[i][:], in1=gain[:], op0=ALU.mult, op1=ALU.mult)
+
+        def weight_turn(i):
+            turned[i] = bank("even")
+            words = weights[i][:].bitcast(F32)
+            for run in range(4):
+                cols = slice(128 * run, 128 * (run + 1))
+                nc.tensor.transpose(turned[i][:, cols], words[:, cols], ident[:])
+
+        def weight_copy(i):
+            weight_cols[i] = rotating([P, S], BF16, "weight_cols", 3)
+            join_words(turned[i], weight_cols[i][:].bitcast(F32), "scalar")
+
+        def weight_quantise(i):
+            weight_mx[i] = (rotating([P, 256], U32, "weight_codes", 6), rotating([P, 256], U8, "weight_scale", 6))
+            codes, scale = weight_mx[i]
+            nc.vector.quantize_mx(out=codes[:].bitcast(FP8X4), scales=scale[:], in_=weight_cols[i][:])
+
+        group_of = {i: (first, count) for first, count in PLANE_GROUPS for i in range(first, first + count)}
+        plane_cols = {}
+
+        def output(i):
+            b, tile_of_batch = divmod(i, TILES_PER_BATCH)
+            codes, scale = weight_mx[i]
+            half_cols = [slice(128 * h, 128 * (h + 1)) for h in range(HALVES)]
+
+            by_row = bank("even")
+            for h in range(HALVES):
+                value_codes, value_scale = value_mx[b, h]
                 nc.tensor.matmul_mx(
-                    out=t[:], lhsT=qc[:, cols].bitcast(FP8X4), lhsT_scale=qs[:, cols], rhs=c[:].bitcast(FP8X4), rhs_scale=s[:], start=True, stop=True
+                    out=by_row[:],
+                    lhsT=codes[:, half_cols[h]].bitcast(FP8X4),
+                    lhsT_scale=scale[:, half_cols[h]],
+                    rhs=value_codes[:].bitcast(FP8X4),
+                    rhs_scale=value_scale[:],
+                    start=(h == 0),
+                    stop=(h == HALVES - 1),
                 )
-                sb[k].append(t)
+            result = rotating([P, C], F32, "result", 4)
+            nc.scalar.copy(out=result[:].rearrange("p (m j) -> p m j", j=4), in_=by_row[:].rearrange("p (j m) -> p m j", j=4))
+            nc.sync.dma_start(out=out_0[b, P * tile_of_batch : P * (tile_of_batch + 1), :], in_=result[:])
 
-        mxt = {}
-
-        def rowmax(k):
-            mx = wt([P, 2], F32, "mx", 3)
-            mxt[k] = mx
-            for gg in range(2):
-                nc.vector.tensor_reduce(out=mx[:, gg : gg + 1], in_=sb[k][gg][:], axis=AX.X, op=ALU.max)
-
-        def shift(k):
-            mx = mxt[k]
-            bias[k] = wt([P, 1], F32, "bias", 3)
-            nc.vector.tensor_scalar(out=bias[k][:], in0=mx[:, 0:1], scalar1=mx[:, 1:2], scalar2=-SCALE, op0=ALU.max, op1=ALU.mult)
-
-        def expo(k):
-            et[k] = wt([P, S], F32, "e", 3)
-            sm = wt([P, 2], F32, "sm", 3)
-            for gg in range(2):
-                nc.scalar.activation(
-                    out=et[k][:, 512 * gg : 512 * (gg + 1)].rearrange("p (u m e) -> p u m e", u=2, e=2),
-                    in_=sb[k][gg][:].rearrange("p (u e m) -> p u m e", u=2, e=2),
-                    func=ACT.Exp,
-                    bias=bias[k][:],
-                    scale=SCALE,
-                    accum_out=sm[:, gg : gg + 1],
-                )
-            tot[k] = wt([P, 1], F32, "tot", 3)
-            nc.scalar.activation(out=tot[k][:], in_=sm[:, 0:1], func=ACT.Identity, bias=sm[:, 1:2])
-
-        rit = {}
-
-        def rec(k):
-            rit[k] = wt([P, 1], F32, "ri", 3)
-            nc.vector.reciprocal(out=rit[k][:], in_=tot[k][:])
-
-        def weights(k):
-            ri = rit[k]
-            at[k] = wt([P, S], BF16, "a", 3)
-            nc.vector.scalar_tensor_tensor(out=at[k][:], in0=et[k][:], scalar=ri[:], in1=bct[:, 0:S], op0=ALU.mult, op1=ALU.mult)
-
-        def a_turn(k):
-            t = bank("a")
-            words = at[k][:].bitcast(F32)
-            for i in range(4):
-                nc.tensor.transpose(t[:, 128 * i : 128 * (i + 1)], words[:, 128 * i : 128 * (i + 1)], ident[:])
-            aT[k] = t
-
-        ag = {}
-
-        def a_copy(k, eng):
-            ag[k] = wt([P, 1024], BF16, "ag", 3)
-            unturn(aT[k], ag[k][:].bitcast(F32), eng)
-
-        def a_quant(k):
-            aq[k] = (wt([P, 256], U32, "aq", 4), wt([P, 256], U8, "aqs", 4))
-            nc.vector.quantize_mx(out=aq[k][0][:].bitcast(FP8X4), scales=aq[k][1][:], in_=ag[k][:])
-
-        def outs_mm(k):
-            b = k // 8
-            ac, as_ = aq[k]
-            o = bank("o")
-            for gg in range(2):
-                c, s = vq[b, gg]
-                cols = slice(128 * gg, 128 * gg + 128)
-                nc.tensor.matmul_mx(
-                    out=o[:], lhsT=ac[:, cols].bitcast(FP8X4), lhsT_scale=as_[:, cols], rhs=c[:].bitcast(FP8X4), rhs_scale=s[:], start=(gg == 0), stop=(gg == 1)
-                )
-            oT = bank("t")
+            by_channel = bank("odd")
             for j in range(4):
-                jc = slice(128 * j, 128 * j + 128)
-                for gg in range(2):
-                    c, s = vq[b, gg]
-                    cols = slice(128 * gg, 128 * gg + 128)
+                cols = slice(128 * j, 128 * (j + 1))
+                for h in range(HALVES):
+                    value_codes, value_scale = value_mx[b, h]
                     nc.tensor.matmul_mx(
-                        out=oT[:, jc], lhsT=c[:, jc].bitcast(FP8X4), lhsT_scale=s[:, jc], rhs=ac[:, cols].bitcast(FP8X4), rhs_scale=as_[:, cols], start=(gg == 0), stop=(gg == 1)
+                        out=by_channel[:, cols],
+                        lhsT=value_codes[:, cols].bitcast(FP8X4),
+                        lhsT_scale=value_scale[:, cols],
+                        rhs=codes[:, half_cols[h]].bitcast(FP8X4),
+                        rhs_scale=scale[:, half_cols[h]],
+                        start=(h == 0),
+                        stop=(h == HALVES - 1),
                     )
-            ob[k] = (o, oT)
-
-        groups = [(0, 4), (4, 4), (8, 4), (12, 2), (14, 1), (15, 1)]
-        group_of = {}
-        for k0, n in groups:
-            for k in range(k0, k0 + n):
-                group_of[k] = (k0, n)
-        pg = {}
-
-        def outs_copy0(k, eng0):
-            o = ob[k][0]
-            b, i = divmod(k, 8)
-            os_ = wt([P, C], F32, "os", 4)
-            copy_on(eng0)(out=os_[:].rearrange("p (m j) -> p m j", j=4), in_=o[:].rearrange("p (j m) -> p m j", j=4))
-            nc.sync.dma_start(out=out_0[b, 128 * i : 128 * (i + 1), :], in_=os_[:])
-
-        def outs_copy1(k, eng1):
-            oT = ob[k][1]
-            k0, n = group_of[k]
-            if k == k0:
-                pg[k0] = wt([P, 512 * n], BF16, "pg%d" % n, 2)
-            copy_on(eng1)(
-                out=pg[k0][:, 512 * (k - k0) : 512 * (k - k0 + 1)].rearrange("p (r j) -> p r j", j=4), in_=oT[:].rearrange("p (j r) -> p r j", j=4)
+            first, count = group_of[i]
+            if i == first:
+                plane_cols[first] = rotating([P, 512 * count], BF16, "plane_cols_%d" % count, 2)
+            copy_with("vector" if i in VECTOR_COPY_TILES else "scalar")(
+                out=plane_cols[first][:, 512 * (i - first) : 512 * (i - first + 1)].rearrange("p (r j) -> p r j", j=4),
+                in_=by_channel[:].rearrange("p (j r) -> p r j", j=4),
             )
 
-        def planes(k):
-            k0, n = group_of[k]
-            if k != k0 + n - 1:
+        def store_planes(i):
+            first, count = group_of[i]
+            if i != first + count - 1:
                 return
-            w = 128 * n
-            pc = wt([P, w], U32, "pc%d" % n, 2)
-            psc = wt([P, w], U8, "psc%d" % n, 2)
-            nc.vector.quantize_mx(out=pc[:].bitcast(FP8X4), scales=psc[:], in_=pg[k0][:])
-            m0 = 128 * k0
-            nc.sync.dma_start(out=out_1[0, :, m0 : m0 + w, :].rearrange("p m t -> p (m t)").bitcast(I32), in_=pc[:].bitcast(I32))
-            for qd in range(4):
-                nc.sync.dma_start(out=out_2[0, 4 * qd : 4 * qd + 4, m0 : m0 + w].bitcast(I32), in_=psc[32 * qd : 32 * qd + 4, :].bitcast(I32))
+            width = P * count
+            codes = rotating([P, width], U32, "plane_codes_%d" % count, 2)
+            scale = rotating([P, width], U8, "plane_scale_%d" % count, 2)
+            nc.vector.quantize_mx(out=codes[:].bitcast(FP8X4), scales=scale[:], in_=plane_cols[first][:])
+            rows = slice(P * first, P * first + width)
+            nc.sync.dma_start(out=out_1[0, :, rows, :].rearrange("p m t -> p (m t)").bitcast(I32), in_=codes[:].bitcast(I32))
+            for quadrant in range(4):
+                nc.sync.dma_start(
+                    out=out_2[0, 4 * quadrant : 4 * quadrant + 4, rows].bitcast(I32),
+                    in_=scale[32 * quadrant : 32 * quadrant + 4, :].bitcast(I32),
+                )
 
-        units = [(b, gg, j) for b in range(B) for gg in range(2) for j in range(4)]
-        unit_at = {-1: [0, 1, 2], 0: [3, 4, 5], 1: [6, 7], 3: [8], 4: [9, 10], 5: [11, 12], 6: [13], 7: [14, 15]}
-        vturn_at = {0: [0], 1: [1, 2], 2: [3], 5: [4], 6: [5], 7: [6], 8: [7]}
-        kc_at = {0: [0, 1], 2: [2, 3]}
-        q_at = {0: 2, 2: 3, 4: 4, 6: 5, 8: 6, 10: 7}
-        outs_at = {k: [k - 1] for k in range(1, NT + 1)}
-        outs_at[1] = []
-        outs_at[2] = []
-        outs_at[3] = [0, 1, 2]
-        spread_at = {1: [4], 3: [5]}
-        kc_parts = [(1, 0, 0), (1, 0, 1), (1, 1, 0), (1, 1, 1)]
-        v_parts = [(b, gg, jp) for b in range(B) for gg in range(2) for jp in range(2)]
+        first_half = [turn(keys[0, 0, n]) for n in range(2)]
+        key_copy(0, 0, 0, first_half[0], "scalar")
+        key_copy(0, 0, 1, first_half[1], "vector")
+        key_quantise(0, 0)
+        column_constants()
+        second_half = [turn(keys[0, 1, n]) for n in range(2)]
+        first_queries = turn(queries[0])
+        key_copy(0, 1, 0, second_half[0], "scalar")
+        key_copy(0, 1, 1, second_half[1], "vector")
+        query_copy(0, first_queries)
+        key_quantise(0, 1)
+        query_quantise(0)
 
-        ta = kc_turn(0, 0, 0)
-        tb = kc_turn(0, 0, 1)
-        kc_copy(0, 0, 0, ta, "s")
-        kc_copy(0, 0, 1, tb, "v")
-        ta = kc_turn(0, 1, 0)
-        tb = kc_turn(0, 1, 1)
-        kc_copy(0, 1, 0, ta, "s")
-        kc_copy(0, 1, 1, tb, "v")
-        ta = q_turn(0)
-        q_copy(0, ta, "s")
-        kc_quant(0, 0)
-        kc_quant(0, 1)
-        q_quant(0)
-        n_perm()
-        scores(0)
-        for i in range(4):
-            ta = spread(i)
-            spread_copy(i, ta, "s")
-        for u in unit_at[-1]:
-            u_mm(*units[u])
-
-        ta = q_turn(1)
-        q_copy(1, ta, "s")
-        pend = [(q_quant, (1,))]
-        for k in range(-1, NT + 3):
-            late = k >= NT - 1
-            if 0 <= k + 2 < NT:
-                scores(k + 2)
-            todo = []
-            for i in kc_at.get(k, []):
-                todo.append((kc_copy, kc_parts[i], kc_turn(*kc_parts[i])))
-            if k in q_at:
-                todo.append((q_copy, (q_at[k],), q_turn(q_at[k])))
-            for i in vturn_at.get(k, []):
-                todo.append((v_copy, v_parts[i], v_turn(*v_parts[i])))
-            for i in spread_at.get(k, []):
-                todo.append((spread_copy, (i,), spread(i)))
-            if k + 1 < NT:
-                rowmax(k + 1)
-            if 0 <= k < NT:
-                rec(k)
-            if 0 <= k - 1 < NT:
-                a_copy(k - 1, "s")
-            for u in unit_at.get(k, [])[:1]:
-                x_stt(*units[u])
-            if k + 1 < NT:
-                shift(k + 1)
-            for u in unit_at.get(k, [])[1:]:
-                x_stt(*units[u])
-            for i in outs_at.get(k - 1, []):
-                outs_copy0(i, "s")
-            for fn, a, t in todo[:1]:
-                fn(*a, t, "s")
-            if k + 1 < NT:
-                expo(k + 1)
-            for i in outs_at.get(k - 1, []):
-                outs_copy1(i, "v" if late else "s")
-            for fn, a, t in todo[1:]:
-                fn(*a, t, "s")
-            if 0 <= k < NT:
-                weights(k)
-            for fn, a in pend:
-                fn(*a)
-            pend = []
-            for u in unit_at.get(k, []):
-                x_sv(*units[u])
-            if 0 <= k - 1 < NT:
-                a_quant(k - 1)
-            for i in outs_at.get(k - 1, []):
-                planes(i)
-            for i in kc_at.get(k, [])[1::2]:
-                pend.append((kc_quant, kc_parts[i][:2]))
-            if k in q_at:
-                pend.append((q_quant, (q_at[k],)))
-            for i in vturn_at.get(k, []):
-                if i % 2 == 1:
-                    pend.append((v_quant, v_parts[i][:2]))
-            for i in outs_at.get(k, []):
-                outs_mm(i)
-            for u in unit_at.get(k + 1, []):
-                u_mm(*units[u])
-            if 0 <= k < NT:
-                a_turn(k)
+        key_quarters = [(1, h, n) for h in range(HALVES) for n in range(2)]
+        for k in range(FIRST_STEP, LAST_STEP + 1):
+            query_turns = [(n, turn(queries[n])) for n in due(QUERY_STEP, k)]
+            for i in query_tile(k - 3):
+                weight_copy(i)
+            for n in due(VALUE_STEP, k - 1):
+                value_sum(n)
+            for i in query_tile(k - 1):
+                exponential(i, 0)
+                exponential(i, 1)
+            for i in query_tile(k):
+                score_max(i, 1)
+            for i in query_tile(k - 3):
+                weight_quantise(i)
+            for n, t in query_turns:
+                query_copy(n, t)
+            if k == GAIN_STEP + 1:
+                for h in range(HALVES):
+                    gain_copy(h, gain_banks[h])
+            for i in query_tile(k - 1):
+                sum_inverse(i)
+            for i in due(OUT_STEP, k):
+                output(i)
+            key_turns = [(n, turn(keys[key_quarters[n]])) for n in due(KEY_STEP, k)]
+            for n, t in query_turns:
+                query_quantise(n)
+            for i in query_tile(k + 1):
+                score_product(i, 0)
+            for n in due(VALUE_STEP, k):
+                beta_key_product(n)
+            for i in query_tile(k - 2):
+                weight_turn(i)
+            for n in due(VALUE_GROUP_STEP, k - 1):
+                value_quantise(*value_groups[n])
+            for i in query_tile(k):
+                score_shift(i)
+            for n, t in key_turns:
+                key_copy(*key_quarters[n], t, "scalar")
+            for n in due(VALUE_GROUP_STEP, k):
+                value_interleave(*value_groups[n])
+            for n, t in key_turns:
+                b, h, quarter = key_quarters[n]
+                if quarter == 1:
+                    key_quantise(b, h)
+            for i in query_tile(k + 1):
+                score_max(i, 0)
+            for i in query_tile(k - 1):
+                weight_product(i)
+            for i in query_tile(k + 1):
+                score_product(i, 1)
+            for n in due(VALUE_STEP, k):
+                beta_key_copy(n)
+            for n in due(VALUE_STEP, k):
+                projection_product(n)
+            if k == GAIN_STEP:
+                gain_banks = [gain_product(h) for h in range(HALVES)]
+            for i in due(OUT_STEP, k):
+                store_planes(i)

import math
from contextlib import ExitStack

import concourse.mybir as mybir
from concourse.masks import make_identity

F32 = mybir.dt.float32
BF16 = mybir.dt.bfloat16
I32 = mybir.dt.int32
U32 = mybir.dt.uint32
U8 = mybir.dt.uint8
FP8X4 = mybir.dt.float8_e4m3fn_x4
ALU = mybir.AluOpType
ACT = mybir.ActivationFunctionType
AX = mybir.AxisListType

B, R, S, C = 2, 1024, 1024, 512
P = 128
HALF = 512
HALVES = S // HALF
TILES = B * R // P
TILES_PER_BATCH = R // P
SCALE = 1.0 / math.sqrt(C)
FLOPS = 2 * B * R * S * C * 2 + 2 * B * S * C * C

QUERY_STEP = [None, 0, 2, 4, 5, 5, 7, 11]
KEY_STEP = [2, 3, 5, 6]
VALUE_STEP = [-2, -2, 0, 0, 1, 1, 2, 3, 3, 4, 4, 5, 6, 7, 9, 10]
VALUE_GROUP_STEP = [1, 4, 8, 11]
GAIN_STEP = 0
OUT_STEP = [7, 8, 9, 9, 10, 11, 12, 12, 13, 14, 15, 15, 16, 17, 18, 19]
FIRST_STEP, LAST_STEP = min(VALUE_STEP), max(OUT_STEP)
VECTOR_COPY_TILES = (11, 12, 14, 15)
PLANE_GROUPS = [(0, 4), (4, 4), (8, 4), (12, 2), (14, 1), (15, 1)]

BANKS = {"score": 4, "even": 2, "odd": 2}


def due(table, step):
    return [n for n, s in enumerate(table) if s == step]


def query_tile(i):
    return [i] if 0 <= i < TILES else []


def tile_mfakeyreusevaluedecode_x2_kernel(tc, q, kc, n_words, n_scales, beta, sv, g, out_0, out_1, out_2):
    nc = tc.nc
    with ExitStack() as ctx:
        keep = ctx.enter_context(tc.tile_pool(name="keep", bufs=1))
        work = ctx.enter_context(tc.tile_pool(name="work", bufs=2))
        psum = ctx.enter_context(tc.psum_pool(name="psum", bufs=1))
        ctx.enter_context(tc.manual_schedule())

        def kept(shape, dtype, name):
            return keep.tile(shape, dtype, name=name, tag=name, align_bytes=64)

        def rotating(shape, dtype, name, bufs):
            return work.tile(shape, dtype, name=name, tag=name, bufs=bufs, align_bytes=64)

        def bank(purpose):
            return psum.tile([P, 512], F32, name=purpose, tag=purpose, bufs=BANKS[purpose])

        def copy_with(engine):
            return nc.scalar.copy if engine == "scalar" else nc.vector.tensor_copy

        gain_row = kept([P, S], BF16, "gain_row")
        ident_bf16 = kept([P, P], BF16, "ident_bf16")
        token_scale_bf16 = kept([P, B * HALVES * 4], BF16, "token_scale_bf16")
        token_scale = kept([P, B * HALVES * 4], F32, "token_scale")
        diag = [kept([P, P], BF16, "diag_%d" % j) for j in range(4)]
        ones = kept([P, P], BF16, "ones")
        n_codes = kept([P, C], U32, "n_codes")
        n_scale = kept([P, C], U8, "n_scale")
        beta_cols = kept([P, 4], BF16, "beta_cols")
        ident = kept([P, P], F32, "ident")
        zeros = kept([P, P], BF16, "zeros")

        nc.gpsimd.memset(n_scale[:].bitcast(I32), 0)
        make_identity(nc, ident[:])
        make_identity(nc, ident_bf16[:])
        nc.vector.memset(zeros[:], 0.0)
        nc.gpsimd.memset(gain_row[:].bitcast(I32), 0)
        nc.scalar.activation(out=ones[:], in_=zeros[:], func=ACT.Exp)

        keys = {}
        queries = {}

        def load_keys(b, h, pieces):
            rows = kc[b, HALF * h : HALF * (h + 1), :].rearrange("(p j) c -> p j c", j=4)
            slots = 4 // pieces
            for piece in range(pieces):
                t = kept([P, slots, C], BF16, "keys_%d%d%d" % (b, h, piece))
                nc.sync.dma_start(out=t[:], in_=rows[:, slots * piece : slots * (piece + 1), :])
                for n in range(slots // 2):
                    keys[b, h, piece * slots // 2 + n] = t[:, 2 * n : 2 * n + 2, :]

        def load_queries(pair):
            t = kept([P, 2, C], BF16, "queries_%d" % pair)
            b, row = divmod(2 * P * pair, R)
            nc.sync.dma_start(out=t[:], in_=q[b, row : row + 2 * P, :].rearrange("(i p) c -> p i c", p=P))
            queries[pair] = t[:]

        load_keys(0, 0, 2)
        load_keys(0, 1, 1)
        load_queries(0)
        nc.sync.dma_start(
            out=token_scale_bf16[:].rearrange("p (a j) -> p a j", j=4),
            in_=sv.rearrange("b t -> (b t)").rearrange("(a p j) -> p a j", p=P, j=4),
        )
        nc.sync.dma_start(out=beta_cols[:], in_=beta.rearrange("(p j) -> p j", j=4))
        nc.sync.dma_start(out=n_codes[:].bitcast(I32), in_=n_words[0].rearrange("p n t -> p (n t)").bitcast(I32))
        for quadrant in range(4):
            nc.sync.dma_start(
                out=n_scale[32 * quadrant : 32 * quadrant + 4, :].bitcast(I32),
                in_=n_scales[0, 4 * quadrant : 4 * quadrant + 4, :].bitcast(I32),
            )
        nc.sync.dma_start(out=gain_row[0:1, :], in_=g.rearrange("(o t) -> o t", o=1))
        for pair in range(1, 4):
            load_queries(pair)
        load_keys(1, 0, 1)
        load_keys(1, 1, 1)
        for pair in range(4, 8):
            load_queries(pair)

        def column_constants():
            nc.vector.tensor_copy(out=token_scale[:], in_=token_scale_bf16[:])
            for j in range(4):
                nc.vector.tensor_scalar(out=diag[j][:], in0=ident_bf16[:], scalar1=beta_cols[:, j : j + 1], scalar2=None, op0=ALU.mult)

        def turn(rows):
            t = bank("odd")
            words = rows.bitcast(F32)
            for n in range(2):
                for u in range(2):
                    nc.tensor.transpose(t[:, 256 * n + 128 * u : 256 * n + 128 * (u + 1)], words[:, n, u:256:2], ident[:])
            return t

        def join_words(t, out_words, engine):
            copy_with(engine)(
                out=out_words.rearrange("p (n r u) -> p n r u", n=2, u=2), in_=t[:].rearrange("p (n u r) -> p n r u", n=2, u=2)
            )

        key_cols = {}
        key_mx = {}
        query_cols = {}
        query_mx = {}
        for b in range(B):
            for h in range(HALVES):
                key_cols[b, h] = kept([P, 4 * HALF], BF16, "key_cols_%d%d" % (b, h))
                key_mx[b, h] = (kept([P, HALF], U32, "key_codes_%d%d" % (b, h)), kept([P, HALF], U8, "key_scale_%d%d" % (b, h)))

        def key_copy(b, h, quarter, t, engine):
            join_words(t, key_cols[b, h][:].bitcast(F32)[:, 512 * quarter : 512 * (quarter + 1)], engine)

        def key_quantise(b, h):
            codes, scale = key_mx[b, h]
            nc.vector.quantize_mx(out=codes[:].bitcast(FP8X4), scales=scale[:], in_=key_cols[b, h][:])

        def query_copy(pair, t):
            query_cols[pair] = rotating([P, 1024], BF16, "query_cols", 3)
            join_words(t, query_cols[pair][:].bitcast(F32), "scalar")

        def query_quantise(pair):
            query_mx[pair] = (kept([P, 256], U32, "query_codes_%d" % pair), kept([P, 256], U8, "query_scale_%d" % pair))
            codes, scale = query_mx[pair]
            nc.vector.quantize_mx(out=codes[:].bitcast(FP8X4), scales=scale[:], in_=query_cols[pair][:])

        gain = kept([P, S], BF16, "gain")

        def gain_product(h):
            t = bank("odd")
            nc.tensor.matmul(t[:], lhsT=ones[:], rhs=gain_row[:, HALF * h : HALF * (h + 1)], start=True, stop=True)
            return t

        def gain_copy(h, t):
            nc.scalar.copy(
                out=gain[:, HALF * h : HALF * (h + 1)].rearrange("p (u k e) -> p u k e", u=2, e=2),
                in_=t[:].rearrange("p (k u e) -> p u k e", u=2, e=2),
            )

        value_slots = [(b, h, j) for b in range(B) for h in range(HALVES) for j in range(4)]
        value_groups = [(b, h) for b in range(B) for h in range(HALVES)]
        beta_key = {}
        scaled_beta_key = {}
        projection = {}
        values = {}
        value_cols = {}
        value_mx = {}
        for b, h in value_groups:
            value_mx[b, h] = (kept([P, C], U32, "value_codes_%d%d" % (b, h)), kept([P, C], U8, "value_scale_%d%d" % (b, h)))

        def beta_key_product(n):
            b, h, slot = value_slots[n]
            beta_key[n] = bank("odd")
            for j in range(4):
                nc.tensor.matmul(
                    beta_key[n][:, 128 * j : 128 * (j + 1)],
                    lhsT=key_cols[b, h][:, 512 * slot + j : 512 * (slot + 1) : 4],
                    rhs=diag[j][:],
                    start=True,
                    stop=True,
                )

        def beta_key_copy(n):
            scaled_beta_key[n] = rotating([P, C], F32, "scaled_beta_key", 3)
            nc.scalar.activation(
                out=scaled_beta_key[n][:].rearrange("p (m j) -> p m j", j=4),
                in_=beta_key[n][:].rearrange("p (j m) -> p m j", j=4),
                func=ACT.Copy,
                scale=token_scale[:, n : n + 1],
            )

        def projection_product(n):
            b, h, slot = value_slots[n]
            projection[n] = bank("even")
            codes, scale = key_mx[b, h]
            cols = slice(128 * slot, 128 * (slot + 1))
            nc.tensor.matmul_mx(
                out=projection[n][:],
                lhsT=codes[:, cols].bitcast(FP8X4),
                lhsT_scale=scale[:, cols],
                rhs=n_codes[:].bitcast(FP8X4),
                rhs_scale=n_scale[:],
                start=True,
                stop=True,
            )

        def value_sum(n):
            b, h, slot = value_slots[n]
            if slot == 0:
                values[b, h] = rotating([P, 4, C], BF16, "values", 2)
            nc.vector.scalar_tensor_tensor(
                out=values[b, h][:, slot, :],
                in0=projection[n][:],
                scalar=token_scale[:, n : n + 1],
                in1=scaled_beta_key[n][:],
                op0=ALU.mult,
                op1=ALU.add,
            )

        def value_interleave(b, h):
            value_cols[b, h] = rotating([P, 4 * C], BF16, "value_cols", 2)
            nc.vector.tensor_copy(
                out=value_cols[b, h][:].rearrange("p (j m t) -> p j m t", j=4, t=4),
                in_=values[b, h][:].rearrange("p t (m j) -> p j m t", j=4),
            )

        def value_quantise(b, h):
            codes, scale = value_mx[b, h]
            nc.vector.quantize_mx(out=codes[:].bitcast(FP8X4), scales=scale[:], in_=value_cols[b, h][:])

        score = {}
        half_max = {}
        shift = {}
        exps = {}
        half_sum = {}
        row_sum = {}
        inverse = {}
        weights = {}
        turned = {}
        weight_cols = {}
        weight_mx = {}

        def score_product(i, h):
            codes, scale = query_mx[i // 2]
            cols = slice(128 * (i % 2), 128 * (i % 2) + 128)
            key_codes, key_scale = key_mx[i // TILES_PER_BATCH, h]
            score[i, h] = bank("score")
            nc.tensor.matmul_mx(
                out=score[i, h][:],
                lhsT=codes[:, cols].bitcast(FP8X4),
                lhsT_scale=scale[:, cols],
                rhs=key_codes[:].bitcast(FP8X4),
                rhs_scale=key_scale[:],
                start=True,
                stop=True,
            )

        def score_max(i, h):
            if h == 0:
                half_max[i] = rotating([P, HALVES], F32, "half_max", 3)
            nc.vector.tensor_reduce(out=half_max[i][:, h : h + 1], in_=score[i, h][:], axis=AX.X, op=ALU.max)

        def score_shift(i):
            shift[i] = rotating([P, 1], F32, "shift", 3)
            nc.vector.tensor_scalar(
                out=shift[i][:], in0=half_max[i][:, 0:1], scalar1=half_max[i][:, 1:2], scalar2=-SCALE, op0=ALU.max, op1=ALU.mult
            )

        def exponential(i, h):
            if h == 0:
                exps[i] = rotating([P, S], F32, "exps", 3)
                half_sum[i] = rotating([P, HALVES], F32, "half_sum", 3)
            nc.scalar.activation(
                out=exps[i][:, HALF * h : HALF * (h + 1)].rearrange("p (u k e) -> p u k e", u=2, e=2),
                in_=score[i, h][:].rearrange("p (u e k) -> p u k e", u=2, e=2),
                func=ACT.Exp,
                bias=shift[i][:],
                scale=SCALE,
                accum_out=half_sum[i][:, h : h + 1],
            )
            if h == HALVES - 1:
                row_sum[i] = rotating([P, 1], F32, "row_sum", 3)
                nc.gpsimd.tensor_tensor(out=row_sum[i][:], in0=half_sum[i][:, 0:1], in1=half_sum[i][:, 1:2], op=ALU.add)

        def sum_inverse(i):
            inverse[i] = rotating([P, 1], F32, "inverse", 3)
            nc.vector.reciprocal(out=inverse[i][:], in_=row_sum[i][:])

        def weight_product(i):
            weights[i] = rotating([P, S], BF16, "weights", 3)
            nc.vector.scalar_tensor_tensor(out=weights[i][:], in0=exps[i][:], scalar=inverse[i][:], in1=gain[:], op0=ALU.mult, op1=ALU.mult)

        def weight_turn(i):
            turned[i] = bank("even")
            words = weights[i][:].bitcast(F32)
            for run in range(4):
                cols = slice(128 * run, 128 * (run + 1))
                nc.tensor.transpose(turned[i][:, cols], words[:, cols], ident[:])

        def weight_copy(i):
            weight_cols[i] = rotating([P, S], BF16, "weight_cols", 3)
            join_words(turned[i], weight_cols[i][:].bitcast(F32), "scalar")

        def weight_quantise(i):
            weight_mx[i] = (rotating([P, 256], U32, "weight_codes", 6), rotating([P, 256], U8, "weight_scale", 6))
            codes, scale = weight_mx[i]
            nc.vector.quantize_mx(out=codes[:].bitcast(FP8X4), scales=scale[:], in_=weight_cols[i][:])

        group_of = {i: (first, count) for first, count in PLANE_GROUPS for i in range(first, first + count)}
        plane_cols = {}

        def output(i):
            b, tile_of_batch = divmod(i, TILES_PER_BATCH)
            codes, scale = weight_mx[i]
            half_cols = [slice(128 * h, 128 * (h + 1)) for h in range(HALVES)]

            by_row = bank("even")
            for h in range(HALVES):
                value_codes, value_scale = value_mx[b, h]
                nc.tensor.matmul_mx(
                    out=by_row[:],
                    lhsT=codes[:, half_cols[h]].bitcast(FP8X4),
                    lhsT_scale=scale[:, half_cols[h]],
                    rhs=value_codes[:].bitcast(FP8X4),
                    rhs_scale=value_scale[:],
                    start=(h == 0),
                    stop=(h == HALVES - 1),
                )
            result = rotating([P, C], F32, "result", 4)
            nc.scalar.copy(out=result[:].rearrange("p (m j) -> p m j", j=4), in_=by_row[:].rearrange("p (j m) -> p m j", j=4))
            nc.sync.dma_start(out=out_0[b, P * tile_of_batch : P * (tile_of_batch + 1), :], in_=result[:])

            by_channel = bank("odd")
            for j in range(4):
                cols = slice(128 * j, 128 * (j + 1))
                for h in range(HALVES):
                    value_codes, value_scale = value_mx[b, h]
                    nc.tensor.matmul_mx(
                        out=by_channel[:, cols],
                        lhsT=value_codes[:, cols].bitcast(FP8X4),
                        lhsT_scale=value_scale[:, cols],
                        rhs=codes[:, half_cols[h]].bitcast(FP8X4),
                        rhs_scale=scale[:, half_cols[h]],
                        start=(h == 0),
                        stop=(h == HALVES - 1),
                    )
            first, count = group_of[i]
            if i == first:
                plane_cols[first] = rotating([P, 512 * count], BF16, "plane_cols_%d" % count, 2)
            copy_with("vector" if i in VECTOR_COPY_TILES else "scalar")(
                out=plane_cols[first][:, 512 * (i - first) : 512 * (i - first + 1)].rearrange("p (r j) -> p r j", j=4),
                in_=by_channel[:].rearrange("p (j r) -> p r j", j=4),
            )

        def store_planes(i):
            first, count = group_of[i]
            if i != first + count - 1:
                return
            width = P * count
            codes = rotating([P, width], U32, "plane_codes_%d" % count, 2)
            scale = rotating([P, width], U8, "plane_scale_%d" % count, 2)
            nc.vector.quantize_mx(out=codes[:].bitcast(FP8X4), scales=scale[:], in_=plane_cols[first][:])
            rows = slice(P * first, P * first + width)
            nc.sync.dma_start(out=out_1[0, :, rows, :].rearrange("p m t -> p (m t)").bitcast(I32), in_=codes[:].bitcast(I32))
            for quadrant in range(4):
                nc.sync.dma_start(
                    out=out_2[0, 4 * quadrant : 4 * quadrant + 4, rows].bitcast(I32),
                    in_=scale[32 * quadrant : 32 * quadrant + 4, :].bitcast(I32),
                )

        first_half = [turn(keys[0, 0, n]) for n in range(2)]
        key_copy(0, 0, 0, first_half[0], "scalar")
        key_copy(0, 0, 1, first_half[1], "vector")
        key_quantise(0, 0)
        column_constants()
        second_half = [turn(keys[0, 1, n]) for n in range(2)]
        first_queries = turn(queries[0])
        key_copy(0, 1, 0, second_half[0], "scalar")
        key_copy(0, 1, 1, second_half[1], "vector")
        query_copy(0, first_queries)
        key_quantise(0, 1)
        query_quantise(0)

        key_quarters = [(1, h, n) for h in range(HALVES) for n in range(2)]
        for k in range(FIRST_STEP, LAST_STEP + 1):
            query_turns = [(n, turn(queries[n])) for n in due(QUERY_STEP, k)]
            for i in query_tile(k - 3):
                weight_copy(i)
            for n in due(VALUE_STEP, k - 1):
                value_sum(n)
            for i in query_tile(k - 1):
                exponential(i, 0)
                exponential(i, 1)
            for i in query_tile(k):
                score_max(i, 1)
            for i in query_tile(k - 3):
                weight_quantise(i)
            for n, t in query_turns:
                query_copy(n, t)
            if k == GAIN_STEP + 1:
                for h in range(HALVES):
                    gain_copy(h, gain_banks[h])
            for i in query_tile(k - 1):
                sum_inverse(i)
            for i in due(OUT_STEP, k):
                output(i)
            key_turns = [(n, turn(keys[key_quarters[n]])) for n in due(KEY_STEP, k)]
            for n, t in query_turns:
                query_quantise(n)
            for i in query_tile(k + 1):
                score_product(i, 0)
            for n in due(VALUE_STEP, k):
                beta_key_product(n)
            for i in query_tile(k - 2):
                weight_turn(i)
            for n in due(VALUE_GROUP_STEP, k - 1):
                value_quantise(*value_groups[n])
            for i in query_tile(k):
                score_shift(i)
            for n, t in key_turns:
                key_copy(*key_quarters[n], t, "scalar")
            for n in due(VALUE_GROUP_STEP, k):
                value_interleave(*value_groups[n])
            for n, t in key_turns:
                b, h, quarter = key_quarters[n]
                if quarter == 1:
                    key_quantise(b, h)
            for i in query_tile(k + 1):
                score_max(i, 0)
            for i in query_tile(k - 1):
                weight_product(i)
            for i in query_tile(k + 1):
                score_product(i, 1)
            for n in due(VALUE_STEP, k):
                beta_key_copy(n)
            for n in due(VALUE_STEP, k):
                projection_product(n)
            if k == GAIN_STEP:
                gain_banks = [gain_product(h) for h in range(HALVES)]
            for i in due(OUT_STEP, k):
                store_planes(i)
